import numpy as np
import ml_dtypes


def mxq(x, axis, fmt="e4m3"):
    dtype, down = {"e4m3": (ml_dtypes.float8_e4m3fn, 7), "e5m2": (ml_dtypes.float8_e5m2, 14)}[fmt]
    v = np.moveaxis(np.asarray(x, np.float32).astype(ml_dtypes.bfloat16).astype(np.float64), axis, -1)
    blocks = v.reshape(v.shape[:-1] + (-1, 32))
    amax = np.abs(blocks).max(-1, keepdims=True)
    byte = np.maximum(np.where(amax > 0, np.frexp(amax)[1] - 1 + 127, 0) - down, 1)
    scale = np.exp2(byte - 127.0)
    codes = (blocks / scale).astype(np.float32).astype(dtype).astype(np.float64)
    return np.moveaxis((codes * scale).reshape(v.shape), -1, axis)


WIDE = False


def mx_kscale(k):
    if not WIDE:
        return np.ones(k)
    levels = np.array([10, -10, 5, -5, 0])
    if k % 512:
        return np.exp2(np.random.permutation(np.resize(levels, k // 32))).repeat(32)
    a = np.empty((k // 512, 16))
    for p in range(k // 512):
        a[p, :8] = np.random.permutation(np.resize(levels, 8))
        for g in range(8):
            far = levels[np.abs(levels - a[p, g]) >= 10]
            a[p, g + 8] = far[np.random.randint(len(far))]
    return np.exp2(a.ravel()).repeat(32)


BF16 = ml_dtypes.bfloat16


def bf(x):
    return np.asarray(x, np.float32).astype(BF16)


def f64(x):
    return np.asarray(x).astype(np.float64)


E2M1 = np.array([0.0, 0.5, 1.0, 1.5, 2.0, 3.0, 4.0, 6.0, -0.0, -0.5, -1.0, -1.5, -2.0, -3.0, -4.0, -6.0])


def pack_weight(w, fmt):
    k, n = w.shape
    w = f64(bf(w)).reshape(k // 32, 32, n)
    amax = np.abs(w).max(1)
    if fmt == "e4m3":
        byte = np.frexp(amax)[1] - 1 + 127 - 7
    else:
        mant, ex = np.frexp(amax / 6.0)
        byte = np.where(mant > 0.5, ex, ex - 1) + 127
    byte = np.clip(np.where(amax > 0, byte, 1), 1, 254)
    scaled = (w * np.exp2(127.0 - byte)[:, None, :]).reshape(k, n).astype(np.float32)
    by_word = np.ascontiguousarray(scaled.reshape(k // 512, 128, 4, n).transpose(0, 1, 3, 2))
    if fmt == "e4m3":
        words = by_word.astype(ml_dtypes.float8_e4m3fn).view(np.uint8)
    else:
        c = by_word.astype(ml_dtypes.float4_e2m1fn).view(np.uint8) & 0xF
        words = c[..., 0::2] | (c[..., 1::2] << 4)
    return np.ascontiguousarray(words), np.ascontiguousarray(byte.astype(np.uint8).reshape(k // 512, 16, n))


def unpack_weight(words, scales, fmt):
    g, p, n, _ = words.shape
    if fmt == "e4m3":
        vals = np.ascontiguousarray(words).view(ml_dtypes.float8_e4m3fn).astype(np.float64)
    else:
        nib = np.empty((g, p, n, 4), np.uint8)
        nib[..., 0::2] = words & 0xF
        nib[..., 1::2] = words >> 4
        vals = E2M1[nib]
    vals = vals * np.repeat(np.exp2(scales.astype(np.float64) - 127.0), 8, axis=1)[..., None]
    return vals.transpose(0, 1, 3, 2).reshape(g * 512, n)


S, F, G, T, C = 1024, 1024, 1024, 512, 512


def smooth_modulus(re, im):
    return np.sqrt(re * re + im * im + 0.25)


def draw0():
    s, t = mx_kscale(S), mx_kscale(F)
    a_scale = 1.0 / np.sqrt(S)
    c_scale = 1.5 / np.sqrt(F)
    x = bf(np.random.standard_normal((S, C)) * s[:, None])
    ar_words, ar_scales = pack_weight((np.random.standard_normal((F, S)) * a_scale / s[None, :]).T, "e4m3")
    aim_words, aim_scales = pack_weight((np.random.standard_normal((F, S)) * a_scale / s[None, :]).T, "e4m3")
    g1 = bf((1.0 + 0.1 * np.random.standard_normal(F)) * t)
    cr_words, cr_scales = pack_weight((np.random.standard_normal((G, F)) * c_scale / t[None, :]).T, "e4m3")
    cim_words, cim_scales = pack_weight((np.random.standard_normal((G, F)) * c_scale / t[None, :]).T, "e4m3")
    phi_words, phi_scales = pack_weight((np.random.standard_normal((T, F)) * c_scale / t[None, :]).T, "e4m3")
    return {
        "x": x,
        "ar_words": ar_words,
        "ar_scales": ar_scales,
        "aim_words": aim_words,
        "aim_scales": aim_scales,
        "g1": g1,
        "cr_words": cr_words,
        "cr_scales": cr_scales,
        "cim_words": cim_words,
        "cim_scales": cim_scales,
        "phi_words": phi_words,
        "phi_scales": phi_scales,
    }


def core(x, ar_words, ar_scales, aim_words, aim_scales, g1, cr_words, cr_scales, cim_words, cim_scales, phi_words, phi_scales):
    xq = mxq(f64(x), 0, "e4m3")
    r1 = unpack_weight(ar_words, ar_scales, "e4m3").T @ xq
    i1 = unpack_weight(aim_words, aim_scales, "e4m3").T @ xq
    u1 = smooth_modulus(r1, i1)
    n1 = f64(g1)[:, None] * (u1 - np.mean(u1, axis=0, keepdims=True))
    nq = mxq(n1, 0, "e4m3")
    s1 = unpack_weight(phi_words, phi_scales, "e4m3").T @ nq
    r2 = unpack_weight(cr_words, cr_scales, "e4m3").T @ nq
    i2 = unpack_weight(cim_words, cim_scales, "e4m3").T @ nq
    u2 = smooth_modulus(r2, i2)
    return s1, u2


def e4m3fn_bytes(y):
    return np.clip(np.asarray(y, np.float64), -448.0, 448.0).astype(np.float32).astype(ml_dtypes.float8_e4m3fn).view(np.uint8)


def e4m3fn_values(b):
    return np.asarray(b, np.uint8).view(ml_dtypes.float8_e4m3fn).astype(np.float64)


def setup_inputs():
    d = draw0()
    x0 = np.asarray(d['x']).astype(np.float64)
    s = (np.max(np.abs(x0), axis=(1,), keepdims=True) / 448.0).astype(np.float32)
    out = {}
    for k, v in d.items():
        if k == 'x':
            out['x_bytes'] = e4m3fn_bytes(x0 / s.astype(np.float64))
            out['x_scale'] = s
        else:
            out[k] = v
    return out


def reference(x_bytes, x_scale, ar_words, ar_scales, aim_words, aim_scales, g1, cr_words, cr_scales, cim_words, cim_scales, phi_words, phi_scales):
    return core(e4m3fn_values(x_bytes) * x_scale.astype(np.float64), ar_words, ar_scales, aim_words, aim_scales, g1, cr_words, cr_scales, cim_words, cim_scales, phi_words, phi_scales)

@@ -1,0 +1,281 @@
+from contextlib import ExitStack
+
+import concourse.mybir as mybir
+from concourse.masks import make_identity
+
+F32 = mybir.dt.float32
+BF16 = mybir.dt.bfloat16
+I32 = mybir.dt.int32
+U32 = mybir.dt.uint32
+U8 = mybir.dt.uint8
+FP8 = mybir.dt.float8_e4m3fn
+FP8X4 = mybir.dt.float8_e4m3fn_x4
+ALU = mybir.AluOpType
+ACT = mybir.ActivationFunctionType
+
+S, F, G, T, C = 1024, 1024, 1024, 512, 512
+P = 128
+NG = 2
+HALF = 512
+NC = C // P
+
+FLOPS = 2 * S * C * (2 * F) + 2 * F * C * (2 * G + T)
+
+UNITS = [("A", 0), ("A", 1), ("A", 2), ("B", 0), ("A", 3), ("B", 1), ("B", 2), ("B", 3)]
+VEC_SQ = ()
+LOOKAHEAD = 2
+
+
+def tile_learnedsecondorderscattering_w8_kernel(
+    tc, x_bytes, x_scale, ar_words, ar_scales, aim_words, aim_scales, g1,
+    cr_words, cr_scales, cim_words, cim_scales, phi_words, phi_scales, out_0, out_1,
+):
+    nc = tc.nc
+    with ExitStack() as ctx:
+        keep = ctx.enter_context(tc.tile_pool(name="keep", bufs=1))
+        work = ctx.enter_context(tc.tile_pool(name="work", bufs=3))
+        psum = ctx.enter_context(tc.psum_pool(name="psum", bufs=1))
+        ctx.enter_context(tc.manual_schedule())
+
+        xs = keep.tile([P, NG, 4], F32, name="xs")
+        nc.sync.dma_start(out=xs[:], in_=x_scale.rearrange("(g p t) o -> p g (t o)", p=P, t=4))
+        x_view = x_bytes.rearrange("(g p t) n -> g p t n", p=P, t=4)
+        xb = []
+        for g in range(NG):
+            xb_g = keep.tile([P, 4, C], U8, name="xb%d" % g)
+            nc.sync.dma_start(out=xb_g[:], in_=x_view[g])
+            xb.append(xb_g)
+
+        pk1 = keep.tile([P, F], U8, name="pk1", align_bytes=64)
+        pk2 = keep.tile([P, G], U8, name="pk2", align_bytes=64)
+        pk3 = keep.tile([P, T], U8, name="pk3", align_bytes=64)
+        nc.vector.memset(pk1[:].bitcast(I32), 0)
+        nc.vector.memset(pk2[:].bitcast(I32), 0)
+        nc.vector.memset(pk3[:].bitcast(I32), 0)
+
+        def load_scales(tile, base, src):
+            for q in range(4):
+                r = 32 * q + base
+                nc.sync.dma_start(out=tile[r : r + 8, :].bitcast(I32), in_=src[:, 4 * q : 4 * q + 4, :].bitcast(I32))
+
+        def load_words(name, src, c0, width):
+            t = keep.tile([P, NG, width], I32, name=name, align_bytes=64)
+            nc.sync.dma_start(
+                out=t[:],
+                in_=src.rearrange("g p n t -> p g (n t)")[:, :, 4 * c0 : 4 * (c0 + width)].bitcast(I32),
+            )
+            return t
+
+        load_scales(pk1, 0, ar_scales)
+        load_scales(pk1, 8, aim_scales)
+        ar, aim, cr, cim = [], [], [], []
+        for h in range(2):
+            ar.append(load_words("ar%d" % h, ar_words, HALF * h, HALF))
+            aim.append(load_words("aim%d" % h, aim_words, HALF * h, HALF))
+        load_scales(pk2, 0, cr_scales)
+        load_scales(pk2, 8, cim_scales)
+        load_scales(pk3, 0, phi_scales)
+        for h in range(2):
+            cr.append(load_words("cr%d" % h, cr_words, HALF * h, HALF))
+            cim.append(load_words("cim%d" % h, cim_words, HALF * h, HALF))
+        phi = load_words("phi", phi_words, 0, T)
+
+        warm = keep.tile([P, 1], F32, name="warm")
+        nc.vector.memset(warm[:], 1.0)
+        nc.scalar.activation(out=warm[:], in_=warm[:], func=ACT.Sqrt)
+        grow = keep.tile([P, F], BF16, name="grow")
+        ones = keep.tile([P, P], BF16, name="ones")
+        nc.vector.memset(grow[:], 0.0)
+        nc.vector.memset(ones[:], 1.0)
+        nc.scalar.dma_start(out=grow[0:1, :], in_=g1.rearrange("(o f) -> o f", o=1))
+        ident = keep.tile([P, P], F32, name="ident")
+        make_identity(nc, ident[:])
+        gb = keep.tile([P, F], BF16, name="gb")
+
+        wid = keep.tile([P, NG, 4, C], BF16, name="wid", align_bytes=64)
+        grp = keep.tile([P, NC, NG, P, 4], BF16, name="grp", align_bytes=64)
+        xc = keep.tile([P, NC, NG, P], U32, name="xc", align_bytes=64)
+        xsc = keep.tile([P, NC, NG, P], U8, name="xsc", align_bytes=64)
+
+        def widen(g, t, c0, c1, eng):
+            src = xb[g][:, t, c0:c1].bitcast(FP8)
+            if eng == "v":
+                nc.vector.tensor_scalar(out=wid[:, g, t, c0:c1], in0=src, scalar1=xs[:, g, t : t + 1], scalar2=None, op0=ALU.mult)
+            else:
+                nc.scalar.activation(out=wid[:, g, t, c0:c1], in_=src, func=ACT.Copy, scale=xs[:, g, t : t + 1])
+
+        def interleave(j, g, eng):
+            dst = grp[:, j, g].rearrange("p (c i) t -> p c t i", i=4)
+            src = wid[:, g, :, P * j : P * (j + 1)].rearrange("p t (c i) -> p c t i", i=4)
+            if eng == "v":
+                nc.vector.tensor_copy(out=dst, in_=src)
+            else:
+                nc.scalar.copy(out=dst, in_=src)
+
+        def quant_x(j):
+            nc.vector.quantize_mx(
+                out=xc[:, j].rearrange("p g c -> p (g c)").bitcast(FP8X4),
+                scales=xsc[:, j].rearrange("p g c -> p (g c)"),
+                in_=grp[:, j].rearrange("p g c t -> p (g c t)"),
+            )
+
+        ncodes, nscales, sums, u1s, n1s, trs, grps = {}, {}, {}, {}, {}, {}, {}
+        banks = {}
+        ss_tiles = {}
+        phis = {}
+        halves = [(kind, j, h) for kind, j in UNITS for h in range(2)]
+
+        def mm_half(k):
+            kind, j, h = halves[k]
+            rb = psum.tile([P, HALF], F32, name="rb", bufs=3)
+            ib = psum.tile([P, HALF], F32, name="ib", bufs=3)
+            banks[k] = (rb, ib)
+            for b, (bank, plane) in enumerate(((rb, 0), (ib, 8))):
+                if kind == "A":
+                    w = (ar, aim)[b][h]
+                    for g in range(NG):
+                        nc.tensor.matmul_mx(
+                            out=bank[:],
+                            lhsT=xc[:, j, g, :].bitcast(FP8X4),
+                            lhsT_scale=xsc[:, j, g, :],
+                            rhs=w[:, g, :].bitcast(FP8X4),
+                            rhs_scale=pk1[plane + 4 * g : P, HALF * h : HALF * (h + 1)],
+                            start=(g == 0), stop=(g == NG - 1),
+                        )
+                else:
+                    w = (cr, cim)[b][h]
+                    mm_out(bank, w, pk2, plane, HALF * h, j)
+            if kind == "B" and h == 0:
+                pb = psum.tile([P, HALF], F32, name="pb", bufs=1)
+                phis[j] = pb
+                mm_out(pb, phi, pk3, 0, 0, j)
+
+        def mm_out(bank, w, pk, plane, s0, j):
+            for q in range(4):
+                for g in range(NG):
+                    nc.tensor.matmul_mx(
+                        out=bank[:, P * q : P * (q + 1)],
+                        lhsT=w[:, g, P * q : P * (q + 1)].bitcast(FP8X4),
+                        lhsT_scale=pk[plane + 4 * g : P, s0 + P * q : s0 + P * (q + 1)],
+                        rhs=ncodes[j][:, g, :].bitcast(FP8X4),
+                        rhs_scale=nscales[j][:, g, :],
+                        start=(g == 0), stop=(g == NG - 1),
+                    )
+
+        def squares(k):
+            rb, ib = banks[k]
+            sr = work.tile([P, HALF], F32, name="sr")
+            si = work.tile([P, HALF], F32, name="si")
+            nc.scalar.activation(out=sr[:], in_=rb[:], func=ACT.Square)
+            if k in VEC_SQ:
+                ic = work.tile([P, HALF], F32, name="ic")
+                nc.vector.tensor_copy(out=ic[:], in_=ib[:])
+                nc.vector.tensor_tensor(out=si[:], in0=ib[:], in1=ic[:], op=ALU.mult)
+            else:
+                nc.scalar.activation(out=si[:], in_=ib[:], func=ACT.Square)
+            return sr, si
+
+        def add(k, sr, si):
+            ss = work.tile([P, HALF], F32, name="ss")
+            nc.vector.scalar_tensor_tensor(out=ss[:], in0=sr[:], scalar=0.25, in1=si[:], op0=ALU.add, op1=ALU.add)
+            ss_tiles[k] = ss
+
+        def root(k):
+            kind, j, h = halves[k]
+            if kind == "A":
+                if h == 0:
+                    u1 = work.tile([P, F], F32, name="u1")
+                    part = work.tile([P, 2], F32, name="part")
+                    u1s[j] = u1
+                    sums[j] = part
+                nc.scalar.activation(out=u1s[j][:, HALF * h : HALF * (h + 1)], in_=ss_tiles[k][:], func=ACT.Sqrt,
+                                     accum_out=sums[j][:, h : h + 1])
+            else:
+                u2 = work.tile([P, 4, P], F32, name="u2")
+                nc.scalar.activation(out=u2[:].rearrange("p q c -> p (q c)"), in_=ss_tiles[k][:], func=ACT.Sqrt)
+                nc.sync.dma_start(
+                    out=out_1.rearrange("(h q m) (j c) -> h j m q c", q=4, m=P, c=P)[h, j], in_=u2[:])
+
+        def centre(j):
+            nm = work.tile([P, 1], F32, name="nm")
+            nc.gpsimd.tensor_scalar(out=nm[:], in0=sums[j][:, 0:1], scalar1=sums[j][:, 1:2], scalar2=-1.0 / F,
+                                    op0=ALU.add, op1=ALU.mult)
+            n1 = work.tile([P, F], BF16, name="n1")
+            nc.vector.scalar_tensor_tensor(out=n1[:], in0=u1s[j][:], scalar=nm[:, 0:1], in1=gb[:], op0=ALU.add, op1=ALU.mult)
+            tr = psum.tile([P, NG, 2, P], F32, name="tr", bufs=1)
+            words = n1[:].bitcast(F32)
+            for g in range(NG):
+                for u in range(2):
+                    nc.tensor.transpose(tr[:, g, u, :], words[:, 256 * g + u : 256 * (g + 1) : 2], ident[:])
+            trs[j] = tr
+
+        def turn(j):
+            gn = work.tile([P, NG, P, 4], BF16, name="gn", align_bytes=64)
+            nc.vector.tensor_copy(out=gn[:].bitcast(F32), in_=trs[j][:].rearrange("p g u c -> p g c u"))
+            grps[j] = gn
+
+        def quant_n(j):
+            codes = work.tile([P, NG, P], U32, name="ncodes", align_bytes=64)
+            scales = work.tile([P, NG, P], U8, name="nscales", align_bytes=64)
+            nc.vector.quantize_mx(
+                out=codes[:].rearrange("p g c -> p (g c)").bitcast(FP8X4),
+                scales=scales[:].rearrange("p g c -> p (g c)"),
+                in_=grps[j][:].rearrange("p g c t -> p (g c t)"),
+            )
+            ncodes[j] = codes
+            nscales[j] = scales
+
+        def store_s1(j):
+            s1 = work.tile([P, 4, P], F32, name="s1")
+            nc.vector.tensor_copy(out=s1[:].rearrange("p q c -> p (q c)"), in_=phis[j][:])
+            nc.sync.dma_start(out=out_0.rearrange("(q m) (j c) -> j m q c", m=P, c=P)[j], in_=s1[:])
+
+        for t in range(4):
+            widen(0, t, 0, P, "v")
+            widen(1, t, 0, P, "s")
+        interleave(0, 0, "v")
+        interleave(0, 1, "v")
+        quant_x(0)
+        for h in range(2):
+            gp = psum.tile([P, HALF], F32, name=("pb", "tr")[h], bufs=1)
+            nc.tensor.matmul(gp[:], lhsT=ones[:], rhs=grow[:, HALF * h : HALF * (h + 1)], start=True, stop=True)
+            nc.scalar.copy(out=gb[:, HALF * h : HALF * (h + 1)], in_=gp[:])
+        mm_half(0)
+        mm_half(1)
+        for t in range(4):
+            widen(0, t, P, C, "v")
+        for t in range(4):
+            widen(1, t, P, C, "v" if t < 1 else "s")
+        interleave(1, 0, "v")
+        interleave(1, 1, "v")
+        quant_x(1)
+
+        last_half = {j: 2 * i + 1 for i, (kind, j) in enumerate(UNITS) if kind == "A"}
+        n_half = len(halves)
+        for k in range(n_half + 1):
+            if k < n_half:
+                sr, si = squares(k)
+            if k >= 1:
+                root(k - 1)
+            for j, a in last_half.items():
+                if k == a + 2:
+                    centre(j)
+                if k == a + 3:
+                    turn(j)
+            if k < n_half:
+                add(k, sr, si)
+            for j, a in last_half.items():
+                if k == a + 3:
+                    quant_n(j)
+            if k < n_half and k >= 1 and halves[k][0] == "B" and halves[k][2] == 1:
+                store_s1(halves[k][1])
+            if k == 0:
+                interleave(2, 0, "v")
+                interleave(2, 1, "v")
+                quant_x(2)
+            if k == 1:
+                interleave(3, 0, "v")
+                interleave(3, 1, "v")
+                quant_x(3)
+            if k + LOOKAHEAD < n_half:
+                mm_half(k + LOOKAHEAD)

@@ -21,8 +21,14 @@ NC = C // P
 
 FLOPS = 2 * S * C * (2 * F) + 2 * F * C * (2 * G + T)
 
-UNITS = [("A", 0), ("A", 1), ("A", 2), ("B", 0), ("A", 3), ("B", 1), ("B", 2), ("B", 3)]
-VEC_SQ = ()
+UNITS = [("A", 0), ("A", 1), ("A", 2), ("A", 3), ("B", 0), ("B", 1), ("B", 2), ("B", 3)]
+VEC_SQ = (3, 12, 14)
+GP_ADD = ()
+ROOT_POS = (1, 1, 1, 1, 1, 2, 2, 1)
+W0 = "ssvvvsss"
+W1 = "svssssvv"
+GAIN_AT = 4
+TURN_AT = 4
 LOOKAHEAD = 2
 
 
@@ -33,7 +39,7 @@ def tile_learnedsecondorderscattering_w8_kernel(
     nc = tc.nc
     with ExitStack() as ctx:
         keep = ctx.enter_context(tc.tile_pool(name="keep", bufs=1))
-        work = ctx.enter_context(tc.tile_pool(name="work", bufs=3))
+        work = ctx.enter_context(tc.tile_pool(name="work", bufs=4))
         psum = ctx.enter_context(tc.psum_pool(name="psum", bufs=1))
         ctx.enter_context(tc.manual_schedule())
 
@@ -45,6 +51,8 @@ def tile_learnedsecondorderscattering_w8_kernel(
             xb_g = keep.tile([P, 4, C], U8, name="xb%d" % g)
             nc.sync.dma_start(out=xb_g[:], in_=x_view[g])
             xb.append(xb_g)
+        gt = keep.tile([P, NG, 4], BF16, name="gt")
+        nc.gpsimd.dma_start(out=gt[:], in_=g1.rearrange("(g p t) -> p g t", p=P, t=4))
 
         pk1 = keep.tile([P, F], U8, name="pk1", align_bytes=64)
         pk2 = keep.tile([P, G], U8, name="pk2", align_bytes=64)
@@ -66,12 +74,13 @@ def tile_learnedsecondorderscattering_w8_kernel(
             )
             return t
 
-        load_scales(pk1, 0, ar_scales)
-        load_scales(pk1, 8, aim_scales)
         ar, aim, cr, cim = [], [], [], []
-        for h in range(2):
-            ar.append(load_words("ar%d" % h, ar_words, HALF * h, HALF))
-            aim.append(load_words("aim%d" % h, aim_words, HALF * h, HALF))
+        load_scales(pk1, 0, ar_scales)
+        ar.append(load_words("ar0", ar_words, 0, HALF))
+        load_scales(pk1, 8, aim_scales)
+        aim.append(load_words("aim0", aim_words, 0, HALF))
+        ar.append(load_words("ar1", ar_words, HALF, HALF))
+        aim.append(load_words("aim1", aim_words, HALF, HALF))
         load_scales(pk2, 0, cr_scales)
         load_scales(pk2, 8, cim_scales)
         load_scales(pk3, 0, phi_scales)
@@ -80,17 +89,12 @@ def tile_learnedsecondorderscattering_w8_kernel(
             cim.append(load_words("cim%d" % h, cim_words, HALF * h, HALF))
         phi = load_words("phi", phi_words, 0, T)
 
+        quarter = keep.tile([P, 1], F32, name="quarter")
+        nc.vector.memset(quarter[:], 0.25)
         warm = keep.tile([P, 1], F32, name="warm")
-        nc.vector.memset(warm[:], 1.0)
-        nc.scalar.activation(out=warm[:], in_=warm[:], func=ACT.Sqrt)
-        grow = keep.tile([P, F], BF16, name="grow")
-        ones = keep.tile([P, P], BF16, name="ones")
-        nc.vector.memset(grow[:], 0.0)
-        nc.vector.memset(ones[:], 1.0)
-        nc.scalar.dma_start(out=grow[0:1, :], in_=g1.rearrange("(o f) -> o f", o=1))
+        nc.scalar.activation(out=warm[:], in_=quarter[:], func=ACT.Sqrt)
         ident = keep.tile([P, P], F32, name="ident")
         make_identity(nc, ident[:])
-        gb = keep.tile([P, F], BF16, name="gb")
 
         wid = keep.tile([P, NG, 4, C], BF16, name="wid", align_bytes=64)
         grp = keep.tile([P, NC, NG, P, 4], BF16, name="grp", align_bytes=64)
@@ -104,13 +108,10 @@ def tile_learnedsecondorderscattering_w8_kernel(
             else:
                 nc.scalar.activation(out=wid[:, g, t, c0:c1], in_=src, func=ACT.Copy, scale=xs[:, g, t : t + 1])
 
-        def interleave(j, g, eng):
+        def interleave(j, g):
             dst = grp[:, j, g].rearrange("p (c i) t -> p c t i", i=4)
             src = wid[:, g, :, P * j : P * (j + 1)].rearrange("p t (c i) -> p c t i", i=4)
-            if eng == "v":
-                nc.vector.tensor_copy(out=dst, in_=src)
-            else:
-                nc.scalar.copy(out=dst, in_=src)
+            nc.vector.tensor_copy(out=dst, in_=src)
 
         def quant_x(j):
             nc.vector.quantize_mx(
@@ -119,10 +120,8 @@ def tile_learnedsecondorderscattering_w8_kernel(
                 in_=grp[:, j].rearrange("p g c t -> p (g c t)"),
             )
 
-        ncodes, nscales, sums, u1s, n1s, trs, grps = {}, {}, {}, {}, {}, {}, {}
-        banks = {}
-        ss_tiles = {}
-        phis = {}
+        ncodes, nscales, sums, u1s, ds, trs, grps = {}, {}, {}, {}, {}, {}, {}
+        banks, ss_tiles, sq_tiles, phis = {}, {}, {}, {}
         halves = [(kind, j, h) for kind, j in UNITS for h in range(2)]
 
         def mm_half(k):
@@ -146,7 +145,7 @@ def tile_learnedsecondorderscattering_w8_kernel(
                     w = (cr, cim)[b][h]
                     mm_out(bank, w, pk2, plane, HALF * h, j)
             if kind == "B" and h == 0:
-                pb = psum.tile([P, HALF], F32, name="pb", bufs=1)
+                pb = psum.tile([P, HALF], F32, name="aux", bufs=2)
                 phis[j] = pb
                 mm_out(pb, phi, pk3, 0, 0, j)
 
@@ -164,54 +163,71 @@ def tile_learnedsecondorderscattering_w8_kernel(
 
         def squares(k):
             rb, ib = banks[k]
-            sr = work.tile([P, HALF], F32, name="sr")
-            si = work.tile([P, HALF], F32, name="si")
-            nc.scalar.activation(out=sr[:], in_=rb[:], func=ACT.Square)
+            u, h = k // 2, k % 2
+            if h == 0:
+                sr = work.tile([P, 2 * HALF], F32, name="sr")
+                si = work.tile([P, 2 * HALF], F32, name="si")
+                sq_tiles[u] = (sr, si)
+            sr, si = sq_tiles[u]
+            cols = slice(HALF * h, HALF * (h + 1))
+            nc.scalar.activation(out=sr[:, cols], in_=rb[:], func=ACT.Square)
+            if h == 1 and ROOT_POS[u - 1] == 2 and u > 0:
+                root(u - 1)
             if k in VEC_SQ:
                 ic = work.tile([P, HALF], F32, name="ic")
                 nc.vector.tensor_copy(out=ic[:], in_=ib[:])
-                nc.vector.tensor_tensor(out=si[:], in0=ib[:], in1=ic[:], op=ALU.mult)
+                nc.vector.tensor_tensor(out=si[:, cols], in0=ib[:], in1=ic[:], op=ALU.mult)
             else:
-                nc.scalar.activation(out=si[:], in_=ib[:], func=ACT.Square)
-            return sr, si
+                nc.scalar.activation(out=si[:, cols], in_=ib[:], func=ACT.Square)
 
-        def add(k, sr, si):
-            ss = work.tile([P, HALF], F32, name="ss")
-            nc.vector.scalar_tensor_tensor(out=ss[:], in0=sr[:], scalar=0.25, in1=si[:], op0=ALU.add, op1=ALU.add)
-            ss_tiles[k] = ss
+        def add(u, c0=0, c1=2 * HALF):
+            sr, si = sq_tiles[u]
+            if c0 == 0:
+                ss = work.tile([P, 2 * HALF], F32, name="ss")
+                ss_tiles[u] = ss
+            eng = nc.gpsimd if u in GP_ADD else nc.vector
+            eng.tensor_tensor(out=ss_tiles[u][:, c0:c1], in0=sr[:, c0:c1], in1=si[:, c0:c1], op=ALU.add)
 
-        def root(k):
-            kind, j, h = halves[k]
+        def root(u, c0=0, c1=2 * HALF):
+            kind, j = UNITS[u]
             if kind == "A":
-                if h == 0:
-                    u1 = work.tile([P, F], F32, name="u1")
-                    part = work.tile([P, 2], F32, name="part")
-                    u1s[j] = u1
-                    sums[j] = part
-                nc.scalar.activation(out=u1s[j][:, HALF * h : HALF * (h + 1)], in_=ss_tiles[k][:], func=ACT.Sqrt,
-                                     accum_out=sums[j][:, h : h + 1])
+                u1 = work.tile([P, F], F32, name="u1")
+                part = work.tile([P, 1], F32, name="part")
+                u1s[j] = u1
+                sums[j] = part
+                nc.scalar.activation(out=u1[:], in_=ss_tiles[u][:], func=ACT.Sqrt, bias=quarter[:], accum_out=part[:])
+                centre(j)
             else:
-                u2 = work.tile([P, 4, P], F32, name="u2")
-                nc.scalar.activation(out=u2[:].rearrange("p q c -> p (q c)"), in_=ss_tiles[k][:], func=ACT.Sqrt)
+                q0, q1 = c0 // P, c1 // P
+                u2 = work.tile([P, q1 - q0, P], F32, name="u2")
+                nc.scalar.activation(out=u2[:].rearrange("p q c -> p (q c)"), in_=ss_tiles[u][:, c0:c1], func=ACT.Sqrt, bias=quarter[:])
                 nc.sync.dma_start(
-                    out=out_1.rearrange("(h q m) (j c) -> h j m q c", q=4, m=P, c=P)[h, j], in_=u2[:])
+                    out=out_1.rearrange("(q m) (j c) -> j m q c", m=P, c=P)[j][:, q0:q1], in_=u2[:])
 
         def centre(j):
             nm = work.tile([P, 1], F32, name="nm")
-            nc.gpsimd.tensor_scalar(out=nm[:], in0=sums[j][:, 0:1], scalar1=sums[j][:, 1:2], scalar2=-1.0 / F,
-                                    op0=ALU.add, op1=ALU.mult)
-            n1 = work.tile([P, F], BF16, name="n1")
-            nc.vector.scalar_tensor_tensor(out=n1[:], in0=u1s[j][:], scalar=nm[:, 0:1], in1=gb[:], op0=ALU.add, op1=ALU.mult)
-            tr = psum.tile([P, NG, 2, P], F32, name="tr", bufs=1)
-            words = n1[:].bitcast(F32)
+            nc.gpsimd.tensor_scalar(out=nm[:], in0=sums[j][:], scalar1=-1.0 / F, scalar2=0.0, op0=ALU.mult, op1=ALU.add)
+            d = work.tile([P, NG, 4, P], F32, name="d")
             for g in range(NG):
-                for u in range(2):
-                    nc.tensor.transpose(tr[:, g, u, :], words[:, 256 * g + u : 256 * (g + 1) : 2], ident[:])
-            trs[j] = tr
+                nc.gpsimd.tensor_scalar(
+                    out=d[:, g], in0=u1s[j][:, 512 * g : 512 * (g + 1)].rearrange("c (p t) -> c t p", t=4),
+                    scalar1=nm[:, 0:1], scalar2=1.0, op0=ALU.add, op1=ALU.mult)
+            ds[j] = d
 
-        def turn(j):
+        def turn_mm(j):
+            trs[j] = []
+            for g in range(NG):
+                tr = psum.tile([P, 4, P], F32, name="aux", bufs=2)
+                for t in range(4):
+                    nc.tensor.transpose(tr[:, t, :], ds[j][:, g, t, :], ident[:])
+                trs[j].append(tr)
+
+        def gain(j):
             gn = work.tile([P, NG, P, 4], BF16, name="gn", align_bytes=64)
-            nc.vector.tensor_copy(out=gn[:].bitcast(F32), in_=trs[j][:].rearrange("p g u c -> p g c u"))
+            for g in range(NG):
+                nc.vector.tensor_tensor(
+                    out=gn[:, g], in0=trs[j][g][:].rearrange("p t c -> p c t"),
+                    in1=gt[:, g, :].unsqueeze(1).to_broadcast([P, P, 4]), op=ALU.mult)
             grps[j] = gn
 
         def quant_n(j):
@@ -230,52 +246,46 @@ def tile_learnedsecondorderscattering_w8_kernel(
             nc.vector.tensor_copy(out=s1[:].rearrange("p q c -> p (q c)"), in_=phis[j][:])
             nc.sync.dma_start(out=out_0.rearrange("(q m) (j c) -> j m q c", m=P, c=P)[j], in_=s1[:])
 
-        for t in range(4):
-            widen(0, t, 0, P, "v")
-            widen(1, t, 0, P, "s")
-        interleave(0, 0, "v")
-        interleave(0, 1, "v")
+        for g in range(NG):
+            for t in range(4):
+                widen(g, t, 0, P, W0[4 * g + t])
+        interleave(0, 0)
+        interleave(0, 1)
         quant_x(0)
-        for h in range(2):
-            gp = psum.tile([P, HALF], F32, name=("pb", "tr")[h], bufs=1)
-            nc.tensor.matmul(gp[:], lhsT=ones[:], rhs=grow[:, HALF * h : HALF * (h + 1)], start=True, stop=True)
-            nc.scalar.copy(out=gb[:, HALF * h : HALF * (h + 1)], in_=gp[:])
         mm_half(0)
         mm_half(1)
-        for t in range(4):
-            widen(0, t, P, C, "v")
-        for t in range(4):
-            widen(1, t, P, C, "v" if t < 1 else "s")
-        interleave(1, 0, "v")
-        interleave(1, 1, "v")
+        for g in range(NG):
+            for t in range(4):
+                widen(g, t, P, C, W1[4 * g + t])
+        interleave(1, 0)
+        interleave(1, 1)
         quant_x(1)
 
-        last_half = {j: 2 * i + 1 for i, (kind, j) in enumerate(UNITS) if kind == "A"}
         n_half = len(halves)
-        for k in range(n_half + 1):
-            if k < n_half:
-                sr, si = squares(k)
-            if k >= 1:
-                root(k - 1)
-            for j, a in last_half.items():
-                if k == a + 2:
-                    centre(j)
-                if k == a + 3:
-                    turn(j)
-            if k < n_half:
-                add(k, sr, si)
-            for j, a in last_half.items():
-                if k == a + 3:
-                    quant_n(j)
-            if k < n_half and k >= 1 and halves[k][0] == "B" and halves[k][2] == 1:
-                store_s1(halves[k][1])
-            if k == 0:
-                interleave(2, 0, "v")
-                interleave(2, 1, "v")
-                quant_x(2)
-            if k == 1:
-                interleave(3, 0, "v")
-                interleave(3, 1, "v")
-                quant_x(3)
+        n_unit = len(UNITS)
+        a_unit = {u: j for u, (kind, j) in enumerate(UNITS) if kind == "A"}
+        for k in range(n_half):
+            u, h = k // 2, k % 2
+            if h == 0 and u > 0:
+                add(u - 1)
+            squares(k)
+            if h == 0 and u > 0 and ROOT_POS[u - 1] == 1:
+                root(u - 1)
+            if k - GAIN_AT >= 0 and (k - GAIN_AT) % 2 == 0 and (k - GAIN_AT) // 2 in a_unit:
+                gain(a_unit[(k - GAIN_AT) // 2])
+            if k - GAIN_AT - 1 >= 0 and (k - GAIN_AT - 1) % 2 == 0 and (k - GAIN_AT - 1) // 2 in a_unit:
+                quant_n(a_unit[(k - GAIN_AT - 1) // 2])
+            if h == 1 and UNITS[u][0] == "B":
+                store_s1(UNITS[u][1])
+            if k < 2:
+                interleave(2 + k, 0)
+                interleave(2 + k, 1)
+                quant_x(2 + k)
             if k + LOOKAHEAD < n_half:
                 mm_half(k + LOOKAHEAD)
+            if k + 1 - TURN_AT >= 0 and (k + 1 - TURN_AT) % 2 == 0 and (k + 1 - TURN_AT) // 2 in a_unit:
+                turn_mm(a_unit[(k + 1 - TURN_AT) // 2])
+            if k == n_half - 1:
+                for c0 in range(0, 2 * HALF, HALF):
+                    add(u, c0, c0 + HALF)
+                    root(u, c0, c0 + HALF)

@@ -22,14 +22,14 @@ NC = C // P
 FLOPS = 2 * S * C * (2 * F) + 2 * F * C * (2 * G + T)
 
 UNITS = [("A", 0), ("A", 1), ("A", 2), ("A", 3), ("B", 0), ("B", 1), ("B", 2), ("B", 3)]
-VEC_SQ = (3, 12, 14)
+VEC_SQ = (6,)
+W0 = "sssvvsss"
+W1 = "svsssvsv"
 GP_ADD = ()
-ROOT_POS = (1, 1, 1, 1, 1, 2, 2, 1)
-W0 = "ssvvvsss"
-W1 = "svssssvv"
-GAIN_AT = 4
-TURN_AT = 4
+CROSS = False
+DUMMIES = 10
 LOOKAHEAD = 2
+PAIR = 2 * HALF
 
 
 def tile_learnedsecondorderscattering_w8_kernel(
@@ -39,7 +39,7 @@ def tile_learnedsecondorderscattering_w8_kernel(
     nc = tc.nc
     with ExitStack() as ctx:
         keep = ctx.enter_context(tc.tile_pool(name="keep", bufs=1))
-        work = ctx.enter_context(tc.tile_pool(name="work", bufs=4))
+        work = ctx.enter_context(tc.tile_pool(name="work", bufs=3))
         psum = ctx.enter_context(tc.psum_pool(name="psum", bufs=1))
         ctx.enter_context(tc.manual_schedule())
 
@@ -51,19 +51,21 @@ def tile_learnedsecondorderscattering_w8_kernel(
             xb_g = keep.tile([P, 4, C], U8, name="xb%d" % g)
             nc.sync.dma_start(out=xb_g[:], in_=x_view[g])
             xb.append(xb_g)
-        gt = keep.tile([P, NG, 4], BF16, name="gt")
-        nc.gpsimd.dma_start(out=gt[:], in_=g1.rearrange("(g p t) -> p g t", p=P, t=4))
 
-        pk1 = keep.tile([P, F], U8, name="pk1", align_bytes=64)
-        pk2 = keep.tile([P, G], U8, name="pk2", align_bytes=64)
-        pk3 = keep.tile([P, T], U8, name="pk3", align_bytes=64)
-        nc.vector.memset(pk1[:].bitcast(I32), 0)
-        nc.vector.memset(pk2[:].bitcast(I32), 0)
-        nc.vector.memset(pk3[:].bitcast(I32), 0)
+        pk_ar, pk_aim, pk_cr, pk_cim, pk_phi = [
+            keep.tile([P, n], U8, name="pk%d" % i, align_bytes=64) for i, n in enumerate((F, F, G, G, T))]
+        quarter = keep.tile([P, 1], F32, name="quarter")
+        nc.vector.memset(quarter[:], 0.25)
+        nc.vector.memset(pk_ar[:].bitcast(I32), 0)
+        nc.vector.memset(pk_aim[:].bitcast(I32), 0)
+        ones = keep.tile([P, HALF], BF16, name="ones")
+        nc.vector.memset(ones[:], 0.0)
+        for pk in (pk_cr, pk_cim, pk_phi):
+            nc.vector.memset(pk[:].bitcast(I32), 0)
 
-        def load_scales(tile, base, src):
+        def load_scales(tile, src):
             for q in range(4):
-                r = 32 * q + base
+                r = 32 * q
                 nc.sync.dma_start(out=tile[r : r + 8, :].bitcast(I32), in_=src[:, 4 * q : 4 * q + 4, :].bitcast(I32))
 
         def load_words(name, src, c0, width):
@@ -75,26 +77,31 @@ def tile_learnedsecondorderscattering_w8_kernel(
             return t
 
         ar, aim, cr, cim = [], [], [], []
-        load_scales(pk1, 0, ar_scales)
+        load_scales(pk_ar, ar_scales)
         ar.append(load_words("ar0", ar_words, 0, HALF))
-        load_scales(pk1, 8, aim_scales)
-        aim.append(load_words("aim0", aim_words, 0, HALF))
         ar.append(load_words("ar1", ar_words, HALF, HALF))
+        load_scales(pk_aim, aim_scales)
+        aim.append(load_words("aim0", aim_words, 0, HALF))
         aim.append(load_words("aim1", aim_words, HALF, HALF))
-        load_scales(pk2, 0, cr_scales)
-        load_scales(pk2, 8, cim_scales)
-        load_scales(pk3, 0, phi_scales)
+        gb = keep.tile([P, F], BF16, name="gb")
+        nc.sync.dma_start(out=gb[:], in_=g1.partition_broadcast(P))
+        load_scales(pk_cr, cr_scales)
+        load_scales(pk_phi, phi_scales)
+        load_scales(pk_cim, cim_scales)
         for h in range(2):
             cr.append(load_words("cr%d" % h, cr_words, HALF * h, HALF))
-            cim.append(load_words("cim%d" % h, cim_words, HALF * h, HALF))
         phi = load_words("phi", phi_words, 0, T)
+        for h in range(2):
+            cim.append(load_words("cim%d" % h, cim_words, HALF * h, HALF))
 
-        quarter = keep.tile([P, 1], F32, name="quarter")
-        nc.vector.memset(quarter[:], 0.25)
         warm = keep.tile([P, 1], F32, name="warm")
         nc.scalar.activation(out=warm[:], in_=quarter[:], func=ACT.Sqrt)
         ident = keep.tile([P, P], F32, name="ident")
         make_identity(nc, ident[:])
+        if DUMMIES:
+            dp = psum.tile([P, HALF], F32, name="aux", bufs=2)
+            for i in range(DUMMIES):
+                nc.tensor.matmul(dp[:], lhsT=ones[:, 0:P], rhs=ones[:], start=True, stop=True)
 
         wid = keep.tile([P, NG, 4, C], BF16, name="wid", align_bytes=64)
         grp = keep.tile([P, NC, NG, P, 4], BF16, name="grp", align_bytes=64)
@@ -120,114 +127,102 @@ def tile_learnedsecondorderscattering_w8_kernel(
                 in_=grp[:, j].rearrange("p g c t -> p (g c t)"),
             )
 
-        ncodes, nscales, sums, u1s, ds, trs, grps = {}, {}, {}, {}, {}, {}, {}
-        banks, ss_tiles, sq_tiles, phis = {}, {}, {}, {}
-        halves = [(kind, j, h) for kind, j in UNITS for h in range(2)]
+        banks, sqs, sss, u1s, sums, nms, n1s, trs, grps, ncodes, nscales, phis = ({} for i in range(12))
 
-        def mm_half(k):
-            kind, j, h = halves[k]
-            rb = psum.tile([P, HALF], F32, name="rb", bufs=3)
-            ib = psum.tile([P, HALF], F32, name="ib", bufs=3)
-            banks[k] = (rb, ib)
-            for b, (bank, plane) in enumerate(((rb, 0), (ib, 8))):
-                if kind == "A":
-                    w = (ar, aim)[b][h]
-                    for g in range(NG):
-                        nc.tensor.matmul_mx(
-                            out=bank[:],
-                            lhsT=xc[:, j, g, :].bitcast(FP8X4),
-                            lhsT_scale=xsc[:, j, g, :],
-                            rhs=w[:, g, :].bitcast(FP8X4),
-                            rhs_scale=pk1[plane + 4 * g : P, HALF * h : HALF * (h + 1)],
-                            start=(g == 0), stop=(g == NG - 1),
-                        )
-                else:
-                    w = (cr, cim)[b][h]
-                    mm_out(bank, w, pk2, plane, HALF * h, j)
-            if kind == "B" and h == 0:
-                pb = psum.tile([P, HALF], F32, name="aux", bufs=2)
-                phis[j] = pb
-                mm_out(pb, phi, pk3, 0, 0, j)
-
-        def mm_out(bank, w, pk, plane, s0, j):
+        def mm_out(bank, w, pk, s0, j):
             for q in range(4):
                 for g in range(NG):
                     nc.tensor.matmul_mx(
                         out=bank[:, P * q : P * (q + 1)],
                         lhsT=w[:, g, P * q : P * (q + 1)].bitcast(FP8X4),
-                        lhsT_scale=pk[plane + 4 * g : P, s0 + P * q : s0 + P * (q + 1)],
+                        lhsT_scale=pk[4 * g : P, s0 + P * q : s0 + P * (q + 1)],
                         rhs=ncodes[j][:, g, :].bitcast(FP8X4),
                         rhs_scale=nscales[j][:, g, :],
                         start=(g == 0), stop=(g == NG - 1),
                     )
 
-        def squares(k):
-            rb, ib = banks[k]
-            u, h = k // 2, k % 2
-            if h == 0:
-                sr = work.tile([P, 2 * HALF], F32, name="sr")
-                si = work.tile([P, 2 * HALF], F32, name="si")
-                sq_tiles[u] = (sr, si)
-            sr, si = sq_tiles[u]
-            cols = slice(HALF * h, HALF * (h + 1))
-            nc.scalar.activation(out=sr[:, cols], in_=rb[:], func=ACT.Square)
-            if h == 1 and ROOT_POS[u - 1] == 2 and u > 0:
-                root(u - 1)
-            if k in VEC_SQ:
-                ic = work.tile([P, HALF], F32, name="ic")
-                nc.vector.tensor_copy(out=ic[:], in_=ib[:])
-                nc.vector.tensor_tensor(out=si[:, cols], in0=ib[:], in1=ic[:], op=ALU.mult)
-            else:
-                nc.scalar.activation(out=si[:, cols], in_=ib[:], func=ACT.Square)
+        def mm_pair(m):
+            u, b = m // 2, m % 2
+            kind, j = UNITS[u]
+            pair = psum.tile([P, 2, HALF], F32, name="pair", bufs=3)
+            banks[m] = pair
+            for h in range(2):
+                if kind == "A":
+                    for g in range(NG):
+                        nc.tensor.matmul_mx(
+                            out=pair[:, h, :],
+                            lhsT=xc[:, j, g, :].bitcast(FP8X4),
+                            lhsT_scale=xsc[:, j, g, :],
+                            rhs=(ar, aim)[b][h][:, g, :].bitcast(FP8X4),
+                            rhs_scale=(pk_ar, pk_aim)[b][4 * g : P, HALF * h : HALF * (h + 1)],
+                            start=(g == 0), stop=(g == NG - 1),
+                        )
+                else:
+                    mm_out(pair[:, h, :], (cr, cim)[b][h], (pk_cr, pk_cim)[b], HALF * h, j)
+            if kind == "B" and b == 0:
+                pb = psum.tile([P, HALF], F32, name="aux", bufs=2)
+                phis[j] = pb
+                mm_out(pb, phi, pk_phi, 0, j)
 
-        def add(u, c0=0, c1=2 * HALF):
-            sr, si = sq_tiles[u]
+        def square_cols(m, c0, c1):
+            src = banks[m][:].rearrange("p h f -> p (h f)")[:, c0:c1]
+            nc.scalar.activation(out=sqs[m][:, c0:c1], in_=src, func=ACT.Square)
+
+        def square(m, parts):
+            sq = work.tile([P, PAIR], F32, name=("sr", "si")[m % 2])
+            sqs[m] = sq
+            for c0, c1 in parts:
+                square_cols(m, c0, c1)
+
+        def vec_square(m):
+            ic = work.tile([P, HALF], F32, name="ic")
+            src = banks[m][:, 1, :]
+            nc.vector.tensor_copy(out=ic[:], in_=src)
+            nc.vector.tensor_tensor(out=sqs[m][:, HALF:PAIR], in0=src, in1=ic[:], op=ALU.mult)
+
+        def add(u, c0=0, c1=PAIR):
             if c0 == 0:
-                ss = work.tile([P, 2 * HALF], F32, name="ss")
-                ss_tiles[u] = ss
+                ss = work.tile([P, PAIR], F32, name="ss")
+                sss[u] = ss
             eng = nc.gpsimd if u in GP_ADD else nc.vector
-            eng.tensor_tensor(out=ss_tiles[u][:, c0:c1], in0=sr[:, c0:c1], in1=si[:, c0:c1], op=ALU.add)
+            eng.tensor_tensor(out=sss[u][:, c0:c1], in0=sqs[2 * u][:, c0:c1], in1=sqs[2 * u + 1][:, c0:c1], op=ALU.add)
 
-        def root(u, c0=0, c1=2 * HALF):
+        def root(u, c0=0, c1=PAIR):
             kind, j = UNITS[u]
             if kind == "A":
                 u1 = work.tile([P, F], F32, name="u1")
                 part = work.tile([P, 1], F32, name="part")
                 u1s[j] = u1
                 sums[j] = part
-                nc.scalar.activation(out=u1[:], in_=ss_tiles[u][:], func=ACT.Sqrt, bias=quarter[:], accum_out=part[:])
-                centre(j)
+                nc.scalar.activation(out=u1[:], in_=sss[u][:], func=ACT.Sqrt, bias=quarter[:], accum_out=part[:])
             else:
-                q0, q1 = c0 // P, c1 // P
-                u2 = work.tile([P, q1 - q0, P], F32, name="u2")
-                nc.scalar.activation(out=u2[:].rearrange("p q c -> p (q c)"), in_=ss_tiles[u][:, c0:c1], func=ACT.Sqrt, bias=quarter[:])
+                n = c1 - c0
+                u2 = work.tile([P, n // P, P], F32, name="u2", bufs=6)
+                nc.scalar.activation(out=u2[:].rearrange("p q c -> p (q c)"), in_=sss[u][:, c0:c1], func=ACT.Sqrt, bias=quarter[:])
                 nc.sync.dma_start(
-                    out=out_1.rearrange("(q m) (j c) -> j m q c", m=P, c=P)[j][:, q0:q1], in_=u2[:])
+                    out=out_1.rearrange("(q m) (j c) -> j m q c", m=P, c=P)[j][:, c0 // P : c1 // P], in_=u2[:])
 
         def centre(j):
             nm = work.tile([P, 1], F32, name="nm")
-            nc.gpsimd.tensor_scalar(out=nm[:], in0=sums[j][:], scalar1=-1.0 / F, scalar2=0.0, op0=ALU.mult, op1=ALU.add)
-            d = work.tile([P, NG, 4, P], F32, name="d")
-            for g in range(NG):
-                nc.gpsimd.tensor_scalar(
-                    out=d[:, g], in0=u1s[j][:, 512 * g : 512 * (g + 1)].rearrange("c (p t) -> c t p", t=4),
-                    scalar1=nm[:, 0:1], scalar2=1.0, op0=ALU.add, op1=ALU.mult)
-            ds[j] = d
+            nc.vector.tensor_scalar(out=nm[:], in0=sums[j][:], scalar1=-1.0 / F, scalar2=None, op0=ALU.mult)
+            nms[j] = nm
+
+        def normalise(j):
+            n1 = work.tile([P, F], BF16, name="n1")
+            nc.vector.scalar_tensor_tensor(out=n1[:], in0=u1s[j][:], scalar=nms[j][:, 0:1], in1=gb[:], op0=ALU.add, op1=ALU.mult)
+            n1s[j] = n1
 
         def turn_mm(j):
-            trs[j] = []
+            tr = psum.tile([P, NG, 2, P], F32, name="aux", bufs=2)
+            words = n1s[j][:].bitcast(F32)
             for g in range(NG):
-                tr = psum.tile([P, 4, P], F32, name="aux", bufs=2)
-                for t in range(4):
-                    nc.tensor.transpose(tr[:, t, :], ds[j][:, g, t, :], ident[:])
-                trs[j].append(tr)
+                for h in range(2):
+                    nc.tensor.transpose(tr[:, g, h, :], words[:, 256 * g + h : 256 * (g + 1) : 2], ident[:])
+            trs[j] = tr
 
-        def gain(j):
+        def turn(j):
             gn = work.tile([P, NG, P, 4], BF16, name="gn", align_bytes=64)
-            for g in range(NG):
-                nc.vector.tensor_tensor(
-                    out=gn[:, g], in0=trs[j][g][:].rearrange("p t c -> p c t"),
-                    in1=gt[:, g, :].unsqueeze(1).to_broadcast([P, P, 4]), op=ALU.mult)
+            nc.vector.tensor_copy(out=gn[:].bitcast(F32), in_=trs[j][:].rearrange("p g u c -> p g c u"))
             grps[j] = gn
 
         def quant_n(j):
@@ -252,8 +247,8 @@ def tile_learnedsecondorderscattering_w8_kernel(
         interleave(0, 0)
         interleave(0, 1)
         quant_x(0)
-        mm_half(0)
-        mm_half(1)
+        mm_pair(0)
+        mm_pair(1)
         for g in range(NG):
             for t in range(4):
                 widen(g, t, P, C, W1[4 * g + t])
@@ -261,31 +256,48 @@ def tile_learnedsecondorderscattering_w8_kernel(
         interleave(1, 1)
         quant_x(1)
 
-        n_half = len(halves)
         n_unit = len(UNITS)
+        whole = [(0, PAIR)] if CROSS else [(0, HALF), (HALF, PAIR)]
+        split = [(0, HALF), (HALF, PAIR)]
         a_unit = {u: j for u, (kind, j) in enumerate(UNITS) if kind == "A"}
-        for k in range(n_half):
-            u, h = k // 2, k % 2
-            if h == 0 and u > 0:
-                add(u - 1)
-            squares(k)
-            if h == 0 and u > 0 and ROOT_POS[u - 1] == 1:
-                root(u - 1)
-            if k - GAIN_AT >= 0 and (k - GAIN_AT) % 2 == 0 and (k - GAIN_AT) // 2 in a_unit:
-                gain(a_unit[(k - GAIN_AT) // 2])
-            if k - GAIN_AT - 1 >= 0 and (k - GAIN_AT - 1) % 2 == 0 and (k - GAIN_AT - 1) // 2 in a_unit:
-                quant_n(a_unit[(k - GAIN_AT - 1) // 2])
-            if h == 1 and UNITS[u][0] == "B":
+        for u in range(n_unit):
+            last = u == n_unit - 1
+            back = a_unit.get(u - 2)
+            square(2 * u, whole if u else split)
+            if back is not None:
+                centre(back)
+                normalise(back)
+            if u < 2:
+                interleave(2 + u, 0)
+                interleave(2 + u, 1)
+                quant_x(2 + u)
+            if 2 * u + LOOKAHEAD < 2 * n_unit:
+                mm_pair(2 * u + LOOKAHEAD)
+            if back is not None:
+                turn_mm(back)
+            if UNITS[u][0] == "B":
                 store_s1(UNITS[u][1])
-            if k < 2:
-                interleave(2 + k, 0)
-                interleave(2 + k, 1)
-                quant_x(2 + k)
-            if k + LOOKAHEAD < n_half:
-                mm_half(k + LOOKAHEAD)
-            if k + 1 - TURN_AT >= 0 and (k + 1 - TURN_AT) % 2 == 0 and (k + 1 - TURN_AT) // 2 in a_unit:
-                turn_mm(a_unit[(k + 1 - TURN_AT) // 2])
-            if k == n_half - 1:
-                for c0 in range(0, 2 * HALF, HALF):
-                    add(u, c0, c0 + HALF)
-                    root(u, c0, c0 + HALF)
+            if u in VEC_SQ or last:
+                square(2 * u + 1, [(0, HALF)])
+            else:
+                square(2 * u + 1, whole if u else split)
+            if u in VEC_SQ:
+                vec_square(2 * u + 1)
+            if not last:
+                add(u)
+            if back is not None:
+                turn(back)
+                quant_n(back)
+            if u > 0:
+                root(u - 1)
+            if 2 * u + 1 + LOOKAHEAD < 2 * n_unit:
+                mm_pair(2 * u + 1 + LOOKAHEAD)
+        u = n_unit - 1
+        add(u, 0, HALF)
+        for c0 in (HALF, HALF + HALF // 2):
+            if u not in VEC_SQ:
+                square_cols(2 * u + 1, c0, c0 + HALF // 2)
+            add(u, c0, c0 + HALF // 2)
+        root(u, 0, HALF)
+        for c0 in (HALF, HALF + HALF // 2):
+            root(u, c0, c0 + HALF // 2)

@@ -22,11 +22,14 @@ NC = C // P
 FLOPS = 2 * S * C * (2 * F) + 2 * F * C * (2 * G + T)
 
 UNITS = [("A", 0), ("A", 1), ("A", 2), ("A", 3), ("B", 0), ("B", 1), ("B", 2), ("B", 3)]
-VEC_SQ = (6,)
-W0 = "sssvvsss"
-W1 = "svsssvsv"
+VEC_SQ = ()
+PHI_MID = {}
+PHI_END = {4: (0,), 5: (1, 2), 6: (3,)}
+S1_AT = {5: (0,), 6: (1, 2), 7: (3,)}
+S1_END = {}
+CHUNKS = ((0, 256), (256, 512))
+WIDEN = ("vsvsvsvs", "svsvsvsv")
 GP_ADD = ()
-CROSS = False
 DUMMIES = 10
 LOOKAHEAD = 2
 PAIR = 2 * HALF
@@ -44,7 +47,7 @@ def tile_learnedsecondorderscattering_w8_kernel(
         ctx.enter_context(tc.manual_schedule())
 
         xs = keep.tile([P, NG, 4], F32, name="xs")
-        nc.sync.dma_start(out=xs[:], in_=x_scale.rearrange("(g p t) o -> p g (t o)", p=P, t=4))
+        nc.scalar.dma_start(out=xs[:], in_=x_scale.rearrange("(g p t) o -> p g (t o)", p=P, t=4))
         x_view = x_bytes.rearrange("(g p t) n -> g p t n", p=P, t=4)
         xb = []
         for g in range(NG):
@@ -59,7 +62,7 @@ def tile_learnedsecondorderscattering_w8_kernel(
         nc.vector.memset(pk_ar[:].bitcast(I32), 0)
         nc.vector.memset(pk_aim[:].bitcast(I32), 0)
         ones = keep.tile([P, HALF], BF16, name="ones")
-        nc.vector.memset(ones[:], 0.0)
+        nc.vector.memset(ones[:], 1.0)
         for pk in (pk_cr, pk_cim, pk_phi):
             nc.vector.memset(pk[:].bitcast(I32), 0)
 
@@ -76,26 +79,26 @@ def tile_learnedsecondorderscattering_w8_kernel(
             )
             return t
 
-        ar, aim, cr, cim = [], [], [], []
+        ar, aim = [], []
         load_scales(pk_ar, ar_scales)
         ar.append(load_words("ar0", ar_words, 0, HALF))
-        ar.append(load_words("ar1", ar_words, HALF, HALF))
         load_scales(pk_aim, aim_scales)
         aim.append(load_words("aim0", aim_words, 0, HALF))
+        ar.append(load_words("ar1", ar_words, HALF, HALF))
         aim.append(load_words("aim1", aim_words, HALF, HALF))
+        grow = keep.tile([P, F], BF16, name="grow")
+        nc.gpsimd.memset(grow[:], 0.0)
         gb = keep.tile([P, F], BF16, name="gb")
-        nc.sync.dma_start(out=gb[:], in_=g1.partition_broadcast(P))
         load_scales(pk_cr, cr_scales)
-        load_scales(pk_phi, phi_scales)
         load_scales(pk_cim, cim_scales)
-        for h in range(2):
-            cr.append(load_words("cr%d" % h, cr_words, HALF * h, HALF))
+        load_scales(pk_phi, phi_scales)
+        cr = load_words("cr", cr_words, 0, G)
+        cim = load_words("cim", cim_words, 0, G)
         phi = load_words("phi", phi_words, 0, T)
-        for h in range(2):
-            cim.append(load_words("cim%d" % h, cim_words, HALF * h, HALF))
 
         warm = keep.tile([P, 1], F32, name="warm")
         nc.scalar.activation(out=warm[:], in_=quarter[:], func=ACT.Sqrt)
+        nc.scalar.dma_start(out=grow[0:1, :], in_=g1.rearrange("(o f) -> o f", o=1))
         ident = keep.tile([P, P], F32, name="ident")
         make_identity(nc, ident[:])
         if DUMMIES:
@@ -134,35 +137,43 @@ def tile_learnedsecondorderscattering_w8_kernel(
                 for g in range(NG):
                     nc.tensor.matmul_mx(
                         out=bank[:, P * q : P * (q + 1)],
-                        lhsT=w[:, g, P * q : P * (q + 1)].bitcast(FP8X4),
+                        lhsT=w[:, g, s0 + P * q : s0 + P * (q + 1)].bitcast(FP8X4),
                         lhsT_scale=pk[4 * g : P, s0 + P * q : s0 + P * (q + 1)],
                         rhs=ncodes[j][:, g, :].bitcast(FP8X4),
                         rhs_scale=nscales[j][:, g, :],
                         start=(g == 0), stop=(g == NG - 1),
                     )
 
+        def mm_first(bank, j, b, h):
+            for g in range(NG):
+                nc.tensor.matmul_mx(
+                    out=bank,
+                    lhsT=xc[:, j, g, :].bitcast(FP8X4),
+                    lhsT_scale=xsc[:, j, g, :],
+                    rhs=(ar, aim)[b][h][:, g, :].bitcast(FP8X4),
+                    rhs_scale=(pk_ar, pk_aim)[b][4 * g : P, HALF * h : HALF * (h + 1)],
+                    start=(g == 0), stop=(g == NG - 1),
+                )
+
         def mm_pair(m):
             u, b = m // 2, m % 2
             kind, j = UNITS[u]
             pair = psum.tile([P, 2, HALF], F32, name="pair", bufs=3)
             banks[m] = pair
+            if u < 2:
+                for s in range(2):
+                    mm_first(pair[:, s, :], s, b, u)
+                return
             for h in range(2):
                 if kind == "A":
-                    for g in range(NG):
-                        nc.tensor.matmul_mx(
-                            out=pair[:, h, :],
-                            lhsT=xc[:, j, g, :].bitcast(FP8X4),
-                            lhsT_scale=xsc[:, j, g, :],
-                            rhs=(ar, aim)[b][h][:, g, :].bitcast(FP8X4),
-                            rhs_scale=(pk_ar, pk_aim)[b][4 * g : P, HALF * h : HALF * (h + 1)],
-                            start=(g == 0), stop=(g == NG - 1),
-                        )
+                    mm_first(pair[:, h, :], j, b, h)
                 else:
-                    mm_out(pair[:, h, :], (cr, cim)[b][h], (pk_cr, pk_cim)[b], HALF * h, j)
-            if kind == "B" and b == 0:
-                pb = psum.tile([P, HALF], F32, name="aux", bufs=2)
-                phis[j] = pb
-                mm_out(pb, phi, pk_phi, 0, j)
+                    mm_out(pair[:, h, :], (cr, cim)[b], (pk_cr, pk_cim)[b], HALF * h, j)
+
+        def mm_phi(j):
+            pb = psum.tile([P, HALF], F32, name="aux", bufs=2)
+            phis[j] = pb
+            mm_out(pb, phi, pk_phi, 0, j)
 
         def square_cols(m, c0, c1):
             src = banks[m][:].rearrange("p h f -> p (h f)")[:, c0:c1]
@@ -190,7 +201,7 @@ def tile_learnedsecondorderscattering_w8_kernel(
         def root(u, c0=0, c1=PAIR):
             kind, j = UNITS[u]
             if kind == "A":
-                u1 = work.tile([P, F], F32, name="u1")
+                u1 = work.tile([P, F], F32, name="u1", bufs=4)
                 part = work.tile([P, 1], F32, name="part")
                 u1s[j] = u1
                 sums[j] = part
@@ -202,9 +213,21 @@ def tile_learnedsecondorderscattering_w8_kernel(
                 nc.sync.dma_start(
                     out=out_1.rearrange("(q m) (j c) -> j m q c", m=P, c=P)[j][:, c0 // P : c1 // P], in_=u2[:])
 
+        def early_root(h, j):
+            if h == 0:
+                u1 = work.tile([P, F], F32, name="u1", bufs=4)
+                part = work.tile([P, 2], F32, name="part2")
+                u1s[j] = u1
+                sums[j] = part
+            nc.scalar.activation(out=u1s[j][:, HALF * h : HALF * (h + 1)], in_=sss[h][:, HALF * j : HALF * (j + 1)],
+                                 func=ACT.Sqrt, bias=quarter[:], accum_out=sums[j][:, h : h + 1])
+
         def centre(j):
             nm = work.tile([P, 1], F32, name="nm")
-            nc.vector.tensor_scalar(out=nm[:], in0=sums[j][:], scalar1=-1.0 / F, scalar2=None, op0=ALU.mult)
+            if j < 2:
+                nc.vector.tensor_scalar(out=nm[:], in0=sums[j][:, 0:1], scalar1=sums[j][:, 1:2], scalar2=-1.0 / F, op0=ALU.add, op1=ALU.mult)
+            else:
+                nc.vector.tensor_scalar(out=nm[:], in0=sums[j][:], scalar1=-1.0 / F, scalar2=None, op0=ALU.mult)
             nms[j] = nm
 
         def normalise(j):
@@ -226,8 +249,8 @@ def tile_learnedsecondorderscattering_w8_kernel(
             grps[j] = gn
 
         def quant_n(j):
-            codes = work.tile([P, NG, P], U32, name="ncodes", align_bytes=64)
-            scales = work.tile([P, NG, P], U8, name="nscales", align_bytes=64)
+            codes = work.tile([P, NG, P], U32, name="ncodes", bufs=4, align_bytes=64)
+            scales = work.tile([P, NG, P], U8, name="nscales", bufs=4, align_bytes=64)
             nc.vector.quantize_mx(
                 out=codes[:].rearrange("p g c -> p (g c)").bitcast(FP8X4),
                 scales=scales[:].rearrange("p g c -> p (g c)"),
@@ -241,57 +264,89 @@ def tile_learnedsecondorderscattering_w8_kernel(
             nc.vector.tensor_copy(out=s1[:].rearrange("p q c -> p (q c)"), in_=phis[j][:])
             nc.sync.dma_start(out=out_0.rearrange("(q m) (j c) -> j m q c", m=P, c=P)[j], in_=s1[:])
 
-        for g in range(NG):
-            for t in range(4):
-                widen(g, t, 0, P, W0[4 * g + t])
-        interleave(0, 0)
-        interleave(0, 1)
-        quant_x(0)
-        mm_pair(0)
+        def prep(j):
+            interleave(j, 0)
+            interleave(j, 1)
+            quant_x(j)
+
+        for i, ((c0, c1), engines) in enumerate(zip(CHUNKS, WIDEN)):
+            for g in range(NG):
+                for t in range(4):
+                    widen(g, t, c0, c1, engines[4 * g + t])
+            if i == 0:
+                for h in range(2):
+                    gp = psum.tile([P, HALF], F32, name="aux", bufs=2)
+                    nc.tensor.matmul(gp[:], lhsT=ones[:, 0:P], rhs=grow[:, HALF * h : HALF * (h + 1)], start=True, stop=True)
+                    nc.scalar.copy(out=gb[:, HALF * h : HALF * (h + 1)], in_=gp[:])
+                prep(0)
+                prep(1)
+                mm_pair(0)
         mm_pair(1)
-        for g in range(NG):
-            for t in range(4):
-                widen(g, t, P, C, W1[4 * g + t])
-        interleave(1, 0)
-        interleave(1, 1)
-        quant_x(1)
 
         n_unit = len(UNITS)
-        whole = [(0, PAIR)] if CROSS else [(0, HALF), (HALF, PAIR)]
-        split = [(0, HALF), (HALF, PAIR)]
-        a_unit = {u: j for u, (kind, j) in enumerate(UNITS) if kind == "A"}
+        whole = [(0, HALF), (HALF, PAIR)]
         for u in range(n_unit):
             last = u == n_unit - 1
-            back = a_unit.get(u - 2)
-            square(2 * u, whole if u else split)
-            if back is not None:
-                centre(back)
-                normalise(back)
+            if u >= 3:
+                whole = [(HALF, PAIR), (0, HALF)]
+            if u in (1, 2):
+                square(2 * u, [whole[0]])
+                early_root(u - 1, 0)
+                square_cols(2 * u, *whole[1])
+                early_root(u - 1, 1)
+            else:
+                square(2 * u, whole)
             if u < 2:
-                interleave(2 + u, 0)
-                interleave(2 + u, 1)
-                quant_x(2 + u)
+                prep(2 + u)
+            if u == 3:
+                turn(1)
+                quant_n(1)
+            if 2 <= u - 3 < NC:
+                turn(u - 3)
+            if 2 <= u - 2 < NC:
+                centre(u - 2)
+            if 2 <= u - 3 < NC:
+                quant_n(u - 3)
+            if 2 <= u - 2 < NC:
+                normalise(u - 2)
+            if u == 2:
+                centre(0)
+                normalise(0)
+                centre(1)
+                normalise(1)
             if 2 * u + LOOKAHEAD < 2 * n_unit:
                 mm_pair(2 * u + LOOKAHEAD)
-            if back is not None:
-                turn_mm(back)
-            if UNITS[u][0] == "B":
-                store_s1(UNITS[u][1])
+            for j in PHI_MID.get(u, ()):
+                mm_phi(j)
+            if 2 <= u - 2 < NC:
+                turn_mm(u - 2)
+            for j in S1_AT.get(u, ()):
+                store_s1(j)
             if u in VEC_SQ or last:
                 square(2 * u + 1, [(0, HALF)])
             else:
-                square(2 * u + 1, whole if u else split)
+                square(2 * u + 1, whole)
             if u in VEC_SQ:
                 vec_square(2 * u + 1)
-            if not last:
+            if u == 2:
+                mm_pair(7)
+                turn_mm(0)
+                turn(0)
+                quant_n(0)
+                turn_mm(1)
+            if u < 2:
+                add(u, 0, HALF)
+                add(u, HALF, PAIR)
+            elif not last:
                 add(u)
-            if back is not None:
-                turn(back)
-                quant_n(back)
-            if u > 0:
+            if u > 2:
                 root(u - 1)
-            if 2 * u + 1 + LOOKAHEAD < 2 * n_unit:
+            if u != 2 and 2 * u + 1 + LOOKAHEAD < 2 * n_unit:
                 mm_pair(2 * u + 1 + LOOKAHEAD)
+            for j in PHI_END.get(u, ()):
+                mm_phi(j)
+            for j in S1_END.get(u, ()):
+                store_s1(j)
         u = n_unit - 1
         add(u, 0, HALF)
         for c0 in (HALF, HALF + HALF // 2):

@@ -90,10 +90,10 @@ def tile_learnedsecondorderscattering_w8_kernel(
         nc.gpsimd.memset(grow[:], 0.0)
         gb = keep.tile([P, F], BF16, name="gb")
         load_scales(pk_cr, cr_scales)
-        load_scales(pk_cim, cim_scales)
-        load_scales(pk_phi, phi_scales)
         cr = load_words("cr", cr_words, 0, G)
+        load_scales(pk_cim, cim_scales)
         cim = load_words("cim", cim_words, 0, G)
+        load_scales(pk_phi, phi_scales)
         phi = load_words("phi", phi_words, 0, T)
 
         warm = keep.tile([P, 1], F32, name="warm")

from contextlib import ExitStack

import concourse.mybir as mybir
from concourse.masks import make_identity

F32 = mybir.dt.float32
BF16 = mybir.dt.bfloat16
I32 = mybir.dt.int32
U32 = mybir.dt.uint32
U8 = mybir.dt.uint8
FP8 = mybir.dt.float8_e4m3fn
FP8X4 = mybir.dt.float8_e4m3fn_x4
ALU = mybir.AluOpType
ACT = mybir.ActivationFunctionType

S, F, G, T, C = 1024, 1024, 1024, 512, 512
P = 128
NG = 2
HALF = 512
NC = C // P

FLOPS = 2 * S * C * (2 * F) + 2 * F * C * (2 * G + T)

UNITS = [("A", 0), ("A", 1), ("A", 2), ("A", 3), ("B", 0), ("B", 1), ("B", 2), ("B", 3)]
VEC_SQ = ()
PHI_MID = {}
PHI_END = {4: (0,), 5: (1, 2), 6: (3,)}
S1_AT = {5: (0,), 6: (1, 2), 7: (3,)}
S1_END = {}
CHUNKS = ((0, 256), (256, 512))
WIDEN = ("vsvsvsvs", "svsvsvsv")
GP_ADD = ()
DUMMIES = 10
LOOKAHEAD = 2
PAIR = 2 * HALF


def tile_learnedsecondorderscattering_w8_kernel(
    tc, x_bytes, x_scale, ar_words, ar_scales, aim_words, aim_scales, g1,
    cr_words, cr_scales, cim_words, cim_scales, phi_words, phi_scales, out_0, out_1,
):
    nc = tc.nc
    with ExitStack() as ctx:
        keep = ctx.enter_context(tc.tile_pool(name="keep", bufs=1))
        work = ctx.enter_context(tc.tile_pool(name="work", bufs=3))
        psum = ctx.enter_context(tc.psum_pool(name="psum", bufs=1))
        ctx.enter_context(tc.manual_schedule())

        xs = keep.tile([P, NG, 4], F32, name="xs")
        nc.scalar.dma_start(out=xs[:], in_=x_scale.rearrange("(g p t) o -> p g (t o)", p=P, t=4))
        x_view = x_bytes.rearrange("(g p t) n -> g p t n", p=P, t=4)
        xb = []
        for g in range(NG):
            xb_g = keep.tile([P, 4, C], U8, name="xb%d" % g)
            nc.sync.dma_start(out=xb_g[:], in_=x_view[g])
            xb.append(xb_g)

        pk_ar, pk_aim, pk_cr, pk_cim, pk_phi = [
            keep.tile([P, n], U8, name="pk%d" % i, align_bytes=64) for i, n in enumerate((F, F, G, G, T))]
        quarter = keep.tile([P, 1], F32, name="quarter")
        nc.vector.memset(quarter[:], 0.25)
        nc.vector.memset(pk_ar[:].bitcast(I32), 0)
        nc.vector.memset(pk_aim[:].bitcast(I32), 0)
        ones = keep.tile([P, HALF], BF16, name="ones")
        nc.vector.memset(ones[:], 1.0)
        for pk in (pk_cr, pk_cim, pk_phi):
            nc.vector.memset(pk[:].bitcast(I32), 0)

        def load_scales(tile, src):
            for q in range(4):
                r = 32 * q
                nc.sync.dma_start(out=tile[r : r + 8, :].bitcast(I32), in_=src[:, 4 * q : 4 * q + 4, :].bitcast(I32))

        def load_words(name, src, c0, width):
            t = keep.tile([P, NG, width], I32, name=name, align_bytes=64)
            nc.sync.dma_start(
                out=t[:],
                in_=src.rearrange("g p n t -> p g (n t)")[:, :, 4 * c0 : 4 * (c0 + width)].bitcast(I32),
            )
            return t

        ar, aim = [], []
        load_scales(pk_ar, ar_scales)
        ar.append(load_words("ar0", ar_words, 0, HALF))
        load_scales(pk_aim, aim_scales)
        aim.append(load_words("aim0", aim_words, 0, HALF))
        ar.append(load_words("ar1", ar_words, HALF, HALF))
        aim.append(load_words("aim1", aim_words, HALF, HALF))
        grow = keep.tile([P, F], BF16, name="grow")
        nc.gpsimd.memset(grow[:], 0.0)
        gb = keep.tile([P, F], BF16, name="gb")
        load_scales(pk_cr, cr_scales)
        cr = load_words("cr", cr_words, 0, G)
        load_scales(pk_cim, cim_scales)
        cim = load_words("cim", cim_words, 0, G)
        load_scales(pk_phi, phi_scales)
        phi = load_words("phi", phi_words, 0, T)

        warm = keep.tile([P, 1], F32, name="warm")
        nc.scalar.activation(out=warm[:], in_=quarter[:], func=ACT.Sqrt)
        nc.scalar.dma_start(out=grow[0:1, :], in_=g1.rearrange("(o f) -> o f", o=1))
        ident = keep.tile([P, P], F32, name="ident")
        make_identity(nc, ident[:])
        if DUMMIES:
            dp = psum.tile([P, HALF], F32, name="aux", bufs=2)
            for i in range(DUMMIES):
                nc.tensor.matmul(dp[:], lhsT=ones[:, 0:P], rhs=ones[:], start=True, stop=True)

        wid = keep.tile([P, NG, 4, C], BF16, name="wid", align_bytes=64)
        grp = keep.tile([P, NC, NG, P, 4], BF16, name="grp", align_bytes=64)
        xc = keep.tile([P, NC, NG, P], U32, name="xc", align_bytes=64)
        xsc = keep.tile([P, NC, NG, P], U8, name="xsc", align_bytes=64)

        def widen(g, t, c0, c1, eng):
            src = xb[g][:, t, c0:c1].bitcast(FP8)
            if eng == "v":
                nc.vector.tensor_scalar(out=wid[:, g, t, c0:c1], in0=src, scalar1=xs[:, g, t : t + 1], scalar2=None, op0=ALU.mult)
            else:
                nc.scalar.activation(out=wid[:, g, t, c0:c1], in_=src, func=ACT.Copy, scale=xs[:, g, t : t + 1])

        def interleave(j, g):
            dst = grp[:, j, g].rearrange("p (c i) t -> p c t i", i=4)
            src = wid[:, g, :, P * j : P * (j + 1)].rearrange("p t (c i) -> p c t i", i=4)
            nc.vector.tensor_copy(out=dst, in_=src)

        def quant_x(j):
            nc.vector.quantize_mx(
                out=xc[:, j].rearrange("p g c -> p (g c)").bitcast(FP8X4),
                scales=xsc[:, j].rearrange("p g c -> p (g c)"),
                in_=grp[:, j].rearrange("p g c t -> p (g c t)"),
            )

        banks, sqs, sss, u1s, sums, nms, n1s, trs, grps, ncodes, nscales, phis = ({} for i in range(12))

        def mm_out(bank, w, pk, s0, j):
            for q in range(4):
                for g in range(NG):
                    nc.tensor.matmul_mx(
                        out=bank[:, P * q : P * (q + 1)],
                        lhsT=w[:, g, s0 + P * q : s0 + P * (q + 1)].bitcast(FP8X4),
                        lhsT_scale=pk[4 * g : P, s0 + P * q : s0 + P * (q + 1)],
                        rhs=ncodes[j][:, g, :].bitcast(FP8X4),
                        rhs_scale=nscales[j][:, g, :],
                        start=(g == 0), stop=(g == NG - 1),
                    )

        def mm_first(bank, j, b, h):
            for g in range(NG):
                nc.tensor.matmul_mx(
                    out=bank,
                    lhsT=xc[:, j, g, :].bitcast(FP8X4),
                    lhsT_scale=xsc[:, j, g, :],
                    rhs=(ar, aim)[b][h][:, g, :].bitcast(FP8X4),
                    rhs_scale=(pk_ar, pk_aim)[b][4 * g : P, HALF * h : HALF * (h + 1)],
                    start=(g == 0), stop=(g == NG - 1),
                )

        def mm_pair(m):
            u, b = m // 2, m % 2
            kind, j = UNITS[u]
            pair = psum.tile([P, 2, HALF], F32, name="pair", bufs=3)
            banks[m] = pair
            if u < 2:
                for s in range(2):
                    mm_first(pair[:, s, :], s, b, u)
                return
            for h in range(2):
                if kind == "A":
                    mm_first(pair[:, h, :], j, b, h)
                else:
                    mm_out(pair[:, h, :], (cr, cim)[b], (pk_cr, pk_cim)[b], HALF * h, j)

        def mm_phi(j):
            pb = psum.tile([P, HALF], F32, name="aux", bufs=2)
            phis[j] = pb
            mm_out(pb, phi, pk_phi, 0, j)

        def square_cols(m, c0, c1):
            src = banks[m][:].rearrange("p h f -> p (h f)")[:, c0:c1]
            nc.scalar.activation(out=sqs[m][:, c0:c1], in_=src, func=ACT.Square)

        def square(m, parts):
            sq = work.tile([P, PAIR], F32, name=("sr", "si")[m % 2])
            sqs[m] = sq
            for c0, c1 in parts:
                square_cols(m, c0, c1)

        def vec_square(m):
            ic = work.tile([P, HALF], F32, name="ic")
            src = banks[m][:, 1, :]
            nc.vector.tensor_copy(out=ic[:], in_=src)
            nc.vector.tensor_tensor(out=sqs[m][:, HALF:PAIR], in0=src, in1=ic[:], op=ALU.mult)

        def add(u, c0=0, c1=PAIR):
            if c0 == 0:
                ss = work.tile([P, PAIR], F32, name="ss")
                sss[u] = ss
            eng = nc.gpsimd if u in GP_ADD else nc.vector
            eng.tensor_tensor(out=sss[u][:, c0:c1], in0=sqs[2 * u][:, c0:c1], in1=sqs[2 * u + 1][:, c0:c1], op=ALU.add)

        def root(u, c0=0, c1=PAIR):
            kind, j = UNITS[u]
            if kind == "A":
                u1 = work.tile([P, F], F32, name="u1", bufs=4)
                part = work.tile([P, 1], F32, name="part")
                u1s[j] = u1
                sums[j] = part
                nc.scalar.activation(out=u1[:], in_=sss[u][:], func=ACT.Sqrt, bias=quarter[:], accum_out=part[:])
            else:
                n = c1 - c0
                u2 = work.tile([P, n // P, P], F32, name="u2", bufs=6)
                nc.scalar.activation(out=u2[:].rearrange("p q c -> p (q c)"), in_=sss[u][:, c0:c1], func=ACT.Sqrt, bias=quarter[:])
                nc.sync.dma_start(
                    out=out_1.rearrange("(q m) (j c) -> j m q c", m=P, c=P)[j][:, c0 // P : c1 // P], in_=u2[:])

        def early_root(h, j):
            if h == 0:
                u1 = work.tile([P, F], F32, name="u1", bufs=4)
                part = work.tile([P, 2], F32, name="part2")
                u1s[j] = u1
                sums[j] = part
            nc.scalar.activation(out=u1s[j][:, HALF * h : HALF * (h + 1)], in_=sss[h][:, HALF * j : HALF * (j + 1)],
                                 func=ACT.Sqrt, bias=quarter[:], accum_out=sums[j][:, h : h + 1])

        def centre(j):
            nm = work.tile([P, 1], F32, name="nm")
            if j < 2:
                nc.vector.tensor_scalar(out=nm[:], in0=sums[j][:, 0:1], scalar1=sums[j][:, 1:2], scalar2=-1.0 / F, op0=ALU.add, op1=ALU.mult)
            else:
                nc.vector.tensor_scalar(out=nm[:], in0=sums[j][:], scalar1=-1.0 / F, scalar2=None, op0=ALU.mult)
            nms[j] = nm

        def normalise(j):
            n1 = work.tile([P, F], BF16, name="n1")
            nc.vector.scalar_tensor_tensor(out=n1[:], in0=u1s[j][:], scalar=nms[j][:, 0:1], in1=gb[:], op0=ALU.add, op1=ALU.mult)
            n1s[j] = n1

        def turn_mm(j):
            tr = psum.tile([P, NG, 2, P], F32, name="aux", bufs=2)
            words = n1s[j][:].bitcast(F32)
            for g in range(NG):
                for h in range(2):
                    nc.tensor.transpose(tr[:, g, h, :], words[:, 256 * g + h : 256 * (g + 1) : 2], ident[:])
            trs[j] = tr

        def turn(j):
            gn = work.tile([P, NG, P, 4], BF16, name="gn", align_bytes=64)
            nc.vector.tensor_copy(out=gn[:].bitcast(F32), in_=trs[j][:].rearrange("p g u c -> p g c u"))
            grps[j] = gn

        def quant_n(j):
            codes = work.tile([P, NG, P], U32, name="ncodes", bufs=4, align_bytes=64)
            scales = work.tile([P, NG, P], U8, name="nscales", bufs=4, align_bytes=64)
            nc.vector.quantize_mx(
                out=codes[:].rearrange("p g c -> p (g c)").bitcast(FP8X4),
                scales=scales[:].rearrange("p g c -> p (g c)"),
                in_=grps[j][:].rearrange("p g c t -> p (g c t)"),
            )
            ncodes[j] = codes
            nscales[j] = scales

        def store_s1(j):
            s1 = work.tile([P, 4, P], F32, name="s1")
            nc.vector.tensor_copy(out=s1[:].rearrange("p q c -> p (q c)"), in_=phis[j][:])
            nc.sync.dma_start(out=out_0.rearrange("(q m) (j c) -> j m q c", m=P, c=P)[j], in_=s1[:])

        def prep(j):
            interleave(j, 0)
            interleave(j, 1)
            quant_x(j)

        for i, ((c0, c1), engines) in enumerate(zip(CHUNKS, WIDEN)):
            for g in range(NG):
                for t in range(4):
                    widen(g, t, c0, c1, engines[4 * g + t])
            if i == 0:
                for h in range(2):
                    gp = psum.tile([P, HALF], F32, name="aux", bufs=2)
                    nc.tensor.matmul(gp[:], lhsT=ones[:, 0:P], rhs=grow[:, HALF * h : HALF * (h + 1)], start=True, stop=True)
                    nc.scalar.copy(out=gb[:, HALF * h : HALF * (h + 1)], in_=gp[:])
                prep(0)
                prep(1)
                mm_pair(0)
        mm_pair(1)

        n_unit = len(UNITS)
        whole = [(0, HALF), (HALF, PAIR)]
        for u in range(n_unit):
            last = u == n_unit - 1
            if u >= 3:
                whole = [(HALF, PAIR), (0, HALF)]
            if u in (1, 2):
                square(2 * u, [whole[0]])
                early_root(u - 1, 0)
                square_cols(2 * u, *whole[1])
                early_root(u - 1, 1)
            else:
                square(2 * u, whole)
            if u < 2:
                prep(2 + u)
            if u == 3:
                turn(1)
                quant_n(1)
            if 2 <= u - 3 < NC:
                turn(u - 3)
            if 2 <= u - 2 < NC:
                centre(u - 2)
            if 2 <= u - 3 < NC:
                quant_n(u - 3)
            if 2 <= u - 2 < NC:
                normalise(u - 2)
            if u == 2:
                centre(0)
                normalise(0)
                centre(1)
                normalise(1)
            if 2 * u + LOOKAHEAD < 2 * n_unit:
                mm_pair(2 * u + LOOKAHEAD)
            for j in PHI_MID.get(u, ()):
                mm_phi(j)
            if 2 <= u - 2 < NC:
                turn_mm(u - 2)
            for j in S1_AT.get(u, ()):
                store_s1(j)
            if u in VEC_SQ or last:
                square(2 * u + 1, [(0, HALF)])
            else:
                square(2 * u + 1, whole)
            if u in VEC_SQ:
                vec_square(2 * u + 1)
            if u == 2:
                mm_pair(7)
                turn_mm(0)
                turn(0)
                quant_n(0)
                turn_mm(1)
            if u < 2:
                add(u, 0, HALF)
                add(u, HALF, PAIR)
            elif not last:
                add(u)
            if u > 2:
                root(u - 1)
            if u != 2 and 2 * u + 1 + LOOKAHEAD < 2 * n_unit:
                mm_pair(2 * u + 1 + LOOKAHEAD)
            for j in PHI_END.get(u, ()):
                mm_phi(j)
            for j in S1_END.get(u, ()):
                store_s1(j)
        u = n_unit - 1
        add(u, 0, HALF)
        for c0 in (HALF, HALF + HALF // 2):
            if u not in VEC_SQ:
                square_cols(2 * u + 1, c0, c0 + HALF // 2)
            add(u, c0, c0 + HALF // 2)
        root(u, 0, HALF)
        for c0 in (HALF, HALF + HALF // 2):
            root(u, c0, c0 + HALF // 2)
